import numpy as np, ml_dtypes
CORES = [113,118,241,246]
N = 4
import mx_ref
NC, G, NE = 256, 4, 128
C = np.float32(0.037)
EX = [0,0,1,1]
BF = ml_dtypes.bfloat16
def cut(t, i, w=512):
    return t[:, w * i:w * i + w]
def tile(rs):
    return np.stack(rs, axis=2).reshape(128, -1).astype(BF)
def layer(w, X):
    out = []
    for i in range(G):
        for t in range(len(X)):
            p = mx_ref.matmul(mx_ref.quantize(cut(w, len(X) * i + t)), X[t])
            z = p if t == 0 else z + p
        out.append(z)
    return out
def act(Z):
    return [np.maximum(z, 0) * C for z in Z]
def setup_inputs(rng):
    def f(*shape):
        return mx_ref.flush((rng.standard_normal(shape, dtype=np.float32) * np.exp2(rng.integers(-2, 3, shape[:-1] + (1,)))).astype(BF))
    return {"x": f(N, 128, 4 * NC), "w1": f(N, 128, G * 512), "w2": f(N, 128, 512)}
def setup_inputs_blocks(rng):
    d = setup_inputs(rng)
    for k in ("x", "w1", "w2"): d[k] = mx_ref.spread(d[k], rng, 2)
    return d
def setup_inputs_wide(rng):
    d = setup_inputs(rng)
    for k in ("x", "w1", "w2"): d[k] = mx_ref.flush((d[k].astype(np.float32) * np.exp2(rng.integers(-6, 7, (N, 1, 1))).astype(np.float32)).astype(BF))
    return d
def reference(x, w1, w2):
    y = np.zeros((N, 128, NC), np.float32)
    for j in range(N):
        for e in range(2):
            X = mx_ref.quantize(cut(x[j], e, 4 * NE)); z = None
            for r in [r_ for r_ in range(N) if EX[r_] == e]:
                p = mx_ref.matmul(mx_ref.quantize(w2[r]), mx_ref.quantize(tile(act(layer(w1[r], [X])))))
                z = p if z is None else z + p
            y[j][:, NE * e:NE * e + NE] = z
    return {"y": y}

@@ -1,0 +1,163 @@
+from concourse.mybir import dt, AluOpType, ActivationFunctionType
+
+R = 128
+G = 4
+CONST = 0.037
+
+SCRATCH = {
+    "xb": ("sbuf", [128, 8 * R], "bfloat16"),
+    "w1b": ("sbuf", [128, 16 * R], "bfloat16"),
+    "w2b": ("sbuf", [128, 4 * R], "bfloat16"),
+    "xq": ("sbuf", [128, 2 * R], "float8_e4m3fn_x4"),
+    "xs": ("sbuf", [128, 2 * R], "uint8"),
+    "w1q": ("sbuf", [128, 4 * R], "float8_e4m3fn_x4"),
+    "w1s": ("sbuf", [128, 4 * R], "uint8"),
+    "w2q": ("sbuf", [128, R], "float8_e4m3fn_x4"),
+    "w2s": ("sbuf", [128, R], "uint8"),
+    "inq": ("sbuf", [128, 3 * R], "float8_e4m3fn_x4"),
+    "ins": ("sbuf", [128, 3 * R], "uint8"),
+    "h": ("sbuf", [128, 16 * R], "bfloat16"),
+    "hq": ("sbuf", [128, 4 * R], "float8_e4m3fn_x4"),
+    "hs": ("sbuf", [128, 4 * R], "uint8"),
+    "out_q": ("sbuf", [128, R], "float32"),
+    "out_p": ("sbuf", [128, R], "float32"),
+    "sum_c": ("sbuf", [128, R], "float32"),
+    "sum_own": ("sbuf", [128, R], "float32"),
+    "land_c": ("sbuf", [128, R], "float32"),
+    "land_own": ("sbuf", [128, R], "float32"),
+    "land_off": ("sbuf", [128, R], "float32"),
+    "z": ("psum", [128, 4 * 512], "float32"),
+    "o": ("psum", [128, 4 * 512], "float32"),
+}
+SEMAPHORES = (
+    ["l_off", "l_own", "l_wa", "l_wb", "l_v", "k_off", "k_own", "k_v", "sent", "st_own", "st_off"]
+    + ["k_w%d" % b for b in range(G)]
+    + ["z%d_%d" % (k, b) for k in range(4) for b in range(G)]
+    + ["%s%d" % (n, k) for n in ("as", "av", "kh", "o") for k in range(4)]
+    + ["r_p", "r_qc", "r_qs", "r_f", "r_own", "r_c", "r_off", "c_p", "c_q", "s_own", "s_c"]
+)
+
+
+def bits(m):
+    return bin(m).count("1")
+
+
+def rank_program(g, core, T, topo):
+    a = T.rank_of(core)
+    if a is None:
+        return
+    S = T.sem
+    ex = T.tables["EX"]
+    e = ex[a]
+    p = [c for r, c in enumerate(T.cores) if ex[r] == e and r != a][0]
+    q = [c for r, c in enumerate(T.cores) if ex[r] != e and topo.die(c) == topo.die(core)][0]
+    qp = [c for r, c in enumerate(T.cores) if ex[r] != e and c != q][0]
+    m_off = topo.mask(core, q)
+    m_on = topo.mask(core, p)
+    m_own = m_on & ~m_off
+    own = slice(R * e, R * e + R)
+    off = slice(R * (1 - e), R * (1 - e) + R)
+    own4 = slice(4 * own.start, 4 * own.stop)
+    off4 = slice(4 * off.start, 4 * off.stop)
+    sent = [0]
+
+    def put(dst, out, in_, sem, mask):
+        rid, pid = topo.addr(dst, core)
+        g.remote_dma(out_ap=out, in_ap=in_, remote_sem=sem, local_sem=S.sent, pid=pid, routing_id=rid, dma_engine_mask=mask)
+        sent[0] += bits(mask)
+
+    n_off, n_on, n_own = bits(m_off), bits(m_on), bits(m_own)
+    Q, P, Q2 = slice(0, R), slice(R, 2 * R), slice(2 * R, 3 * R)
+
+    g.sync.dma_start(T.xb[:, off4], T.x[:, off4]).then_inc(S.l_off, 16)
+    g.sync.dma_start(T.xb[:, own4], T.x[:, own4]).then_inc(S.l_own, 16)
+    g.sync.dma_start(T.w1b[:, 0:8 * R], T.w1[:, 0:8 * R]).then_inc(S.l_wa, 16)
+    g.sync.dma_start(T.w1b[:, 8 * R:16 * R], T.w1[:, 8 * R:16 * R]).then_inc(S.l_wb, 16)
+    g.sync.dma_start(T.w2b[:], T.w2[:]).then_inc(S.l_v, 16)
+
+    v = g.vector
+    v.wait_ge(S.l_off, 16)
+    v.quantize_mx(T.xq[:, off], T.xs[:, off], T.xb[:, off4]).then_inc(S.k_off, 1)
+    v.wait_ge(S.l_own, 16)
+    v.quantize_mx(T.xq[:, own], T.xs[:, own], T.xb[:, own4]).then_inc(S.k_own, 1)
+    for b in range(G):
+        if b == 0:
+            v.wait_ge(S.l_wa, 16)
+        if b == 2:
+            v.wait_ge(S.l_wb, 16)
+        v.quantize_mx(T.w1q[:, b * R:b * R + R], T.w1s[:, b * R:b * R + R],
+                      T.w1b[:, 4 * b * R:4 * b * R + 4 * R]).then_inc(S["k_w%d" % b], 1)
+    v.wait_ge(S.l_v, 16)
+    v.quantize_mx(T.w2q[:], T.w2s[:], T.w2b[:]).then_inc(S.k_v, 1)
+
+    g.wait_ge(S.k_off, 1)
+    put(q, T.inq[:, Q].bitcast(dt.uint8), T.xq[:, off].bitcast(dt.uint8), S.r_qc, m_off)
+    put(q, T.ins[:, Q], T.xs[:, off], S.r_qs, m_off)
+    g.wait_ge(S.k_own, 1)
+    put(p, T.inq[:, P].bitcast(dt.uint8), T.xq[:, own].bitcast(dt.uint8), S.r_p, m_own)
+    put(p, T.ins[:, P], T.xs[:, own], S.r_p, m_own)
+    g.wait_ge(S.r_qc, n_off)
+    put(p, T.inq[:, Q2].bitcast(dt.uint8), T.inq[:, Q].bitcast(dt.uint8), S.r_f, m_on)
+    g.wait_ge(S.r_qs, n_off)
+    put(p, T.ins[:, Q2], T.ins[:, Q], S.r_f, m_on)
+
+    runs = [
+        (T.inq, T.ins, Q, [(S.r_qc, n_off), (S.r_qs, n_off)]),
+        (T.inq, T.ins, P, [(S.r_p, 2 * n_own)]),
+        (T.inq, T.ins, Q2, [(S.r_f, 2 * n_on)]),
+        (T.xq, T.xs, own, [(S.k_own, 1)]),
+    ]
+    for k, (cq, cs, cols, waits) in enumerate(runs):
+        kc = slice(R * k, R * k + R)
+        o = T.o[:, 512 * k:512 * k + R]
+        for sem, val in waits:
+            g.tensor.wait_ge(sem, val)
+        for b in range(G):
+            if k == 0:
+                g.tensor.wait_ge(S["k_w%d" % b], 1)
+            g.tensor.matmul_mx(T.z[:, 512 * b:512 * b + R], T.w1q[:, b * R:b * R + R], T.w1s[:, b * R:b * R + R],
+                               cq[:, cols], cs[:, cols], True, True).then_inc(S["z%d_%d" % (k, b)], 1)
+        for b in range(G):
+            out = T.h[:, 4 * R * k + b:4 * R * (k + 1):4]
+            src = T.z[:, 512 * b:512 * b + R]
+            if b % 2 == 0:
+                g.scalar.wait_ge(S["z%d_%d" % (k, b)], 1)
+                g.scalar.activation(out, src, ActivationFunctionType.Relu, scale=CONST).then_inc(S["as%d" % k], 1)
+            else:
+                v.wait_ge(S["z%d_%d" % (k, b)], 1)
+                v.tensor_scalar(out, src, 0.0, CONST, AluOpType.max, AluOpType.mult).then_inc(S["av%d" % k], 1)
+        v.wait_ge(S["as%d" % k], 2)
+        v.wait_ge(S["av%d" % k], 2)
+        v.quantize_mx(T.hq[:, kc], T.hs[:, kc], T.h[:, 4 * R * k:4 * R * (k + 1)]).then_inc(S["kh%d" % k], 1)
+        if k == 0:
+            g.tensor.wait_ge(S.k_v, 1)
+        g.tensor.wait_ge(S["kh%d" % k], 1)
+        g.tensor.matmul_mx(o, T.w2q[:], T.w2s[:], T.hq[:, kc], T.hs[:, kc], True, True).then_inc(S["o%d" % k], 1)
+        if k == 0:
+            v.wait_ge(S.o0, 1)
+            v.tensor_copy(T.out_q[:], o).then_inc(S.c_q, 1)
+            g.wait_ge(S.c_q, 1)
+            put(p, T.land_c[:], T.out_q[:], S.r_c, m_on)
+        elif k == 1:
+            g.scalar.wait_ge(S.o1, 1)
+            g.scalar.activation(T.out_p[:], o, ActivationFunctionType.Copy).then_inc(S.c_p, 1)
+            g.wait_ge(S.c_p, 1)
+            put(p, T.land_own[:], T.out_p[:], S.r_own, m_on)
+        elif k == 2:
+            v.wait_ge(S.o2, 1)
+            v.wait_ge(S.r_c, n_on)
+            v.tensor_tensor(T.sum_c[:], o, T.land_c[:], AluOpType.add).then_inc(S.s_c, 1)
+            g.wait_ge(S.s_c, 1)
+            put(qp, T.land_off[:], T.sum_c[:], S.r_off, m_off)
+        else:
+            v.wait_ge(S.o3, 1)
+            v.wait_ge(S.r_own, n_on)
+            v.tensor_tensor(T.sum_own[:], o, T.land_own[:], AluOpType.add).then_inc(S.s_own, 1)
+
+    g.scalar.wait_ge(S.s_own, 1)
+    g.scalar.dma_start(T.y[:, own], T.sum_own[:]).then_inc(S.st_own, 16)
+    g.scalar.wait_ge(S.st_own, 16)
+    g.sync.wait_ge(S.r_off, n_off)
+    g.sync.dma_start(T.y[:, off], T.land_off[:]).then_inc(S.st_off, 16)
+    g.sync.wait_ge(S.st_off, 16)
+    g.wait_ge(S.sent, sent[0])

@@ -32,8 +32,8 @@ SCRATCH = {
 SEMAPHORES = (
     ["l_off", "l_own", "l_wa", "l_wb", "l_v", "k_off", "k_own", "k_v", "sent", "st_own", "st_off"]
     + ["k_w%d" % b for b in range(G)]
-    + ["z%d_%d" % (k, b) for k in range(4) for b in range(G)]
-    + ["%s%d" % (n, k) for n in ("as", "av", "kh", "o") for k in range(4)]
+    + ["%s%d_%d" % (n, k, b) for n in ("z", "h") for k in range(4) for b in range(G)]
+    + ["%s%d" % (n, k) for n in ("kh", "o") for k in range(4)]
     + ["r_p", "r_qc", "r_qs", "r_f", "r_own", "r_c", "r_off", "c_p", "c_q", "s_own", "s_c"]
 )
 
@@ -47,6 +47,7 @@ def rank_program(g, core, T, topo):
     if a is None:
         return
     S = T.sem
+    v = g.vector
     ex = T.tables["EX"]
     e = ex[a]
     p = [c for r, c in enumerate(T.cores) if ex[r] == e and r != a][0]
@@ -75,7 +76,6 @@ def rank_program(g, core, T, topo):
     g.sync.dma_start(T.w1b[:, 8 * R:16 * R], T.w1[:, 8 * R:16 * R]).then_inc(S.l_wb, 16)
     g.sync.dma_start(T.w2b[:], T.w2[:]).then_inc(S.l_v, 16)
 
-    v = g.vector
     v.wait_ge(S.l_off, 16)
     v.quantize_mx(T.xq[:, off], T.xs[:, off], T.xb[:, off4]).then_inc(S.k_off, 1)
     v.wait_ge(S.l_own, 16)
@@ -107,52 +107,73 @@ def rank_program(g, core, T, topo):
         (T.inq, T.ins, Q2, [(S.r_f, 2 * n_on)]),
         (T.xq, T.xs, own, [(S.k_own, 1)]),
     ]
-    for k, (cq, cs, cols, waits) in enumerate(runs):
-        kc = slice(R * k, R * k + R)
-        o = T.o[:, 512 * k:512 * k + R]
+
+    def o(k):
+        return T.o[:, 512 * k:512 * k + R]
+
+    def layer1(k):
+        cq, cs, cols, waits = runs[k]
         for sem, val in waits:
             g.tensor.wait_ge(sem, val)
         for b in range(G):
             if k == 0:
                 g.tensor.wait_ge(S["k_w%d" % b], 1)
+            else:
+                g.tensor.wait_ge(S["h%d_%d" % (k - 1, b)], 1)
             g.tensor.matmul_mx(T.z[:, 512 * b:512 * b + R], T.w1q[:, b * R:b * R + R], T.w1s[:, b * R:b * R + R],
                                cq[:, cols], cs[:, cols], True, True).then_inc(S["z%d_%d" % (k, b)], 1)
+
+    def tile(k):
         for b in range(G):
             out = T.h[:, 4 * R * k + b:4 * R * (k + 1):4]
             src = T.z[:, 512 * b:512 * b + R]
+            z, h = S["z%d_%d" % (k, b)], S["h%d_%d" % (k, b)]
             if b % 2 == 0:
-                g.scalar.wait_ge(S["z%d_%d" % (k, b)], 1)
-                g.scalar.activation(out, src, ActivationFunctionType.Relu, scale=CONST).then_inc(S["as%d" % k], 1)
+                g.scalar.wait_ge(z, 1)
+                g.scalar.activation(out, src, ActivationFunctionType.Relu, scale=CONST).then_inc(h, 1)
             else:
-                v.wait_ge(S["z%d_%d" % (k, b)], 1)
-                v.tensor_scalar(out, src, 0.0, CONST, AluOpType.max, AluOpType.mult).then_inc(S["av%d" % k], 1)
-        v.wait_ge(S["as%d" % k], 2)
-        v.wait_ge(S["av%d" % k], 2)
-        v.quantize_mx(T.hq[:, kc], T.hs[:, kc], T.h[:, 4 * R * k:4 * R * (k + 1)]).then_inc(S["kh%d" % k], 1)
+                v.wait_ge(z, 1)
+                v.tensor_scalar(out, src, 0.0, CONST, AluOpType.max, AluOpType.mult).then_inc(h, 1)
+        for b in range(G):
+            v.wait_ge(S["h%d_%d" % (k, b)], 1)
+        v.quantize_mx(T.hq[:, R * k:R * k + R], T.hs[:, R * k:R * k + R],
+                      T.h[:, 4 * R * k:4 * R * (k + 1)]).then_inc(S["kh%d" % k], 1)
+
+    def layer2(k):
         if k == 0:
             g.tensor.wait_ge(S.k_v, 1)
         g.tensor.wait_ge(S["kh%d" % k], 1)
-        g.tensor.matmul_mx(o, T.w2q[:], T.w2s[:], T.hq[:, kc], T.hs[:, kc], True, True).then_inc(S["o%d" % k], 1)
-        if k == 0:
-            v.wait_ge(S.o0, 1)
-            v.tensor_copy(T.out_q[:], o).then_inc(S.c_q, 1)
-            g.wait_ge(S.c_q, 1)
-            put(p, T.land_c[:], T.out_q[:], S.r_c, m_on)
-        elif k == 1:
-            g.scalar.wait_ge(S.o1, 1)
-            g.scalar.activation(T.out_p[:], o, ActivationFunctionType.Copy).then_inc(S.c_p, 1)
-            g.wait_ge(S.c_p, 1)
-            put(p, T.land_own[:], T.out_p[:], S.r_own, m_on)
-        elif k == 2:
-            v.wait_ge(S.o2, 1)
-            v.wait_ge(S.r_c, n_on)
-            v.tensor_tensor(T.sum_c[:], o, T.land_c[:], AluOpType.add).then_inc(S.s_c, 1)
-            g.wait_ge(S.s_c, 1)
-            put(qp, T.land_off[:], T.sum_c[:], S.r_off, m_off)
-        else:
-            v.wait_ge(S.o3, 1)
-            v.wait_ge(S.r_own, n_on)
-            v.tensor_tensor(T.sum_own[:], o, T.land_own[:], AluOpType.add).then_inc(S.s_own, 1)
+        g.tensor.matmul_mx(o(k), T.w2q[:], T.w2s[:], T.hq[:, R * k:R * k + R], T.hs[:, R * k:R * k + R],
+                           True, True).then_inc(S["o%d" % k], 1)
+
+    layer1(0)
+    tile(0)
+    layer2(0)
+    v.wait_ge(S.o0, 1)
+    v.tensor_copy(T.out_q[:], o(0)).then_inc(S.c_q, 1)
+    g.wait_ge(S.c_q, 1)
+    put(p, T.land_c[:], T.out_q[:], S.r_c, m_on)
+    layer1(1)
+    tile(1)
+    layer1(2)
+    tile(2)
+    layer2(1)
+    g.scalar.wait_ge(S.o1, 1)
+    g.scalar.activation(T.out_p[:], o(1), ActivationFunctionType.Copy).then_inc(S.c_p, 1)
+    g.wait_ge(S.c_p, 1)
+    put(p, T.land_own[:], T.out_p[:], S.r_own, m_on)
+    layer2(2)
+    v.wait_ge(S.o2, 1)
+    v.wait_ge(S.r_c, n_on)
+    v.tensor_tensor(T.sum_c[:], o(2), T.land_c[:], AluOpType.add).then_inc(S.s_c, 1)
+    g.wait_ge(S.s_c, 1)
+    put(qp, T.land_off[:], T.sum_c[:], S.r_off, m_off)
+    layer1(3)
+    tile(3)
+    layer2(3)
+    v.wait_ge(S.o3, 1)
+    v.wait_ge(S.r_own, n_on)
+    v.tensor_tensor(T.sum_own[:], o(3), T.land_own[:], AluOpType.add).then_inc(S.s_own, 1)
 
     g.scalar.wait_ge(S.s_own, 1)
     g.scalar.dma_start(T.y[:, own], T.sum_own[:]).then_inc(S.st_own, 16)

from concourse.mybir import dt, AluOpType, ActivationFunctionType

R = 128
G = 4
CONST = 0.037

SCRATCH = {
    "xb": ("sbuf", [128, 8 * R], "bfloat16"),
    "w1b": ("sbuf", [128, 16 * R], "bfloat16"),
    "w2b": ("sbuf", [128, 4 * R], "bfloat16"),
    "xq": ("sbuf", [128, 2 * R], "float8_e4m3fn_x4"),
    "xs": ("sbuf", [128, 2 * R], "uint8"),
    "w1q": ("sbuf", [128, 4 * R], "float8_e4m3fn_x4"),
    "w1s": ("sbuf", [128, 4 * R], "uint8"),
    "w2q": ("sbuf", [128, R], "float8_e4m3fn_x4"),
    "w2s": ("sbuf", [128, R], "uint8"),
    "inq": ("sbuf", [128, 3 * R], "float8_e4m3fn_x4"),
    "ins": ("sbuf", [128, 3 * R], "uint8"),
    "h": ("sbuf", [128, 16 * R], "bfloat16"),
    "hq": ("sbuf", [128, 4 * R], "float8_e4m3fn_x4"),
    "hs": ("sbuf", [128, 4 * R], "uint8"),
    "out_q": ("sbuf", [128, R], "float32"),
    "out_p": ("sbuf", [128, R], "float32"),
    "sum_c": ("sbuf", [128, R], "float32"),
    "sum_own": ("sbuf", [128, R], "float32"),
    "land_c": ("sbuf", [128, R], "float32"),
    "land_own": ("sbuf", [128, R], "float32"),
    "land_off": ("sbuf", [128, R], "float32"),
    "z": ("psum", [128, 4 * 512], "float32"),
    "o": ("psum", [128, 4 * 512], "float32"),
}
SEMAPHORES = (
    ["l_off", "l_own", "l_wa", "l_wb", "l_v", "k_off", "k_own", "k_v", "sent", "st_own", "st_off"]
    + ["k_w%d" % b for b in range(G)]
    + ["%s%d_%d" % (n, k, b) for n in ("z", "h") for k in range(4) for b in range(G)]
    + ["%s%d" % (n, k) for n in ("kh", "o") for k in range(4)]
    + ["r_p", "r_qc", "r_qs", "r_f", "r_own", "r_c", "r_off", "c_p", "c_q", "s_own", "s_c"]
)


def bits(m):
    return bin(m).count("1")


def rank_program(g, core, T, topo):
    a = T.rank_of(core)
    if a is None:
        return
    S = T.sem
    v = g.vector
    ex = T.tables["EX"]
    e = ex[a]
    p = [c for r, c in enumerate(T.cores) if ex[r] == e and r != a][0]
    q = [c for r, c in enumerate(T.cores) if ex[r] != e and topo.die(c) == topo.die(core)][0]
    qp = [c for r, c in enumerate(T.cores) if ex[r] != e and c != q][0]
    m_off = topo.mask(core, q)
    m_on = topo.mask(core, p)
    m_own = m_on & ~m_off
    own = slice(R * e, R * e + R)
    off = slice(R * (1 - e), R * (1 - e) + R)
    own4 = slice(4 * own.start, 4 * own.stop)
    off4 = slice(4 * off.start, 4 * off.stop)
    sent = [0]

    def put(dst, out, in_, sem, mask):
        rid, pid = topo.addr(dst, core)
        g.remote_dma(out_ap=out, in_ap=in_, remote_sem=sem, local_sem=S.sent, pid=pid, routing_id=rid, dma_engine_mask=mask)
        sent[0] += bits(mask)

    n_off, n_on, n_own = bits(m_off), bits(m_on), bits(m_own)
    Q, P, Q2 = slice(0, R), slice(R, 2 * R), slice(2 * R, 3 * R)

    g.sync.dma_start(T.xb[:, off4], T.x[:, off4]).then_inc(S.l_off, 16)
    g.sync.dma_start(T.xb[:, own4], T.x[:, own4]).then_inc(S.l_own, 16)
    g.sync.dma_start(T.w1b[:, 0:8 * R], T.w1[:, 0:8 * R]).then_inc(S.l_wa, 16)
    g.sync.dma_start(T.w1b[:, 8 * R:16 * R], T.w1[:, 8 * R:16 * R]).then_inc(S.l_wb, 16)
    g.sync.dma_start(T.w2b[:], T.w2[:]).then_inc(S.l_v, 16)

    v.wait_ge(S.l_off, 16)
    v.quantize_mx(T.xq[:, off], T.xs[:, off], T.xb[:, off4]).then_inc(S.k_off, 1)
    v.wait_ge(S.l_own, 16)
    v.quantize_mx(T.xq[:, own], T.xs[:, own], T.xb[:, own4]).then_inc(S.k_own, 1)
    for b in range(G):
        if b == 0:
            v.wait_ge(S.l_wa, 16)
        if b == 2:
            v.wait_ge(S.l_wb, 16)
        v.quantize_mx(T.w1q[:, b * R:b * R + R], T.w1s[:, b * R:b * R + R],
                      T.w1b[:, 4 * b * R:4 * b * R + 4 * R]).then_inc(S["k_w%d" % b], 1)
    v.wait_ge(S.l_v, 16)
    v.quantize_mx(T.w2q[:], T.w2s[:], T.w2b[:]).then_inc(S.k_v, 1)

    g.wait_ge(S.k_off, 1)
    put(q, T.inq[:, Q].bitcast(dt.uint8), T.xq[:, off].bitcast(dt.uint8), S.r_qc, m_off)
    put(q, T.ins[:, Q], T.xs[:, off], S.r_qs, m_off)
    g.wait_ge(S.k_own, 1)
    put(p, T.inq[:, P].bitcast(dt.uint8), T.xq[:, own].bitcast(dt.uint8), S.r_p, m_own)
    put(p, T.ins[:, P], T.xs[:, own], S.r_p, m_own)
    g.wait_ge(S.r_qc, n_off)
    put(p, T.inq[:, Q2].bitcast(dt.uint8), T.inq[:, Q].bitcast(dt.uint8), S.r_f, m_on)
    g.wait_ge(S.r_qs, n_off)
    put(p, T.ins[:, Q2], T.ins[:, Q], S.r_f, m_on)

    runs = [
        (T.inq, T.ins, Q, [(S.r_qc, n_off), (S.r_qs, n_off)]),
        (T.inq, T.ins, P, [(S.r_p, 2 * n_own)]),
        (T.inq, T.ins, Q2, [(S.r_f, 2 * n_on)]),
        (T.xq, T.xs, own, [(S.k_own, 1)]),
    ]

    def o(k):
        return T.o[:, 512 * k:512 * k + R]

    def layer1(k):
        cq, cs, cols, waits = runs[k]
        for sem, val in waits:
            g.tensor.wait_ge(sem, val)
        for b in range(G):
            if k == 0:
                g.tensor.wait_ge(S["k_w%d" % b], 1)
            else:
                g.tensor.wait_ge(S["h%d_%d" % (k - 1, b)], 1)
            g.tensor.matmul_mx(T.z[:, 512 * b:512 * b + R], T.w1q[:, b * R:b * R + R], T.w1s[:, b * R:b * R + R],
                               cq[:, cols], cs[:, cols], True, True).then_inc(S["z%d_%d" % (k, b)], 1)

    def tile(k):
        for b in range(G):
            out = T.h[:, 4 * R * k + b:4 * R * (k + 1):4]
            src = T.z[:, 512 * b:512 * b + R]
            z, h = S["z%d_%d" % (k, b)], S["h%d_%d" % (k, b)]
            if b % 2 == 0:
                g.scalar.wait_ge(z, 1)
                g.scalar.activation(out, src, ActivationFunctionType.Relu, scale=CONST).then_inc(h, 1)
            else:
                v.wait_ge(z, 1)
                v.tensor_scalar(out, src, 0.0, CONST, AluOpType.max, AluOpType.mult).then_inc(h, 1)
        for b in range(G):
            v.wait_ge(S["h%d_%d" % (k, b)], 1)
        v.quantize_mx(T.hq[:, R * k:R * k + R], T.hs[:, R * k:R * k + R],
                      T.h[:, 4 * R * k:4 * R * (k + 1)]).then_inc(S["kh%d" % k], 1)

    def layer2(k):
        if k == 0:
            g.tensor.wait_ge(S.k_v, 1)
        g.tensor.wait_ge(S["kh%d" % k], 1)
        g.tensor.matmul_mx(o(k), T.w2q[:], T.w2s[:], T.hq[:, R * k:R * k + R], T.hs[:, R * k:R * k + R],
                           True, True).then_inc(S["o%d" % k], 1)

    layer1(0)
    tile(0)
    layer2(0)
    v.wait_ge(S.o0, 1)
    v.tensor_copy(T.out_q[:], o(0)).then_inc(S.c_q, 1)
    g.wait_ge(S.c_q, 1)
    put(p, T.land_c[:], T.out_q[:], S.r_c, m_on)
    layer1(1)
    tile(1)
    layer1(2)
    tile(2)
    layer2(1)
    g.scalar.wait_ge(S.o1, 1)
    g.scalar.activation(T.out_p[:], o(1), ActivationFunctionType.Copy).then_inc(S.c_p, 1)
    g.wait_ge(S.c_p, 1)
    put(p, T.land_own[:], T.out_p[:], S.r_own, m_on)
    layer2(2)
    v.wait_ge(S.o2, 1)
    v.wait_ge(S.r_c, n_on)
    v.tensor_tensor(T.sum_c[:], o(2), T.land_c[:], AluOpType.add).then_inc(S.s_c, 1)
    g.wait_ge(S.s_c, 1)
    put(qp, T.land_off[:], T.sum_c[:], S.r_off, m_off)
    layer1(3)
    tile(3)
    layer2(3)
    v.wait_ge(S.o3, 1)
    v.wait_ge(S.r_own, n_on)
    v.tensor_tensor(T.sum_own[:], o(3), T.land_own[:], AluOpType.add).then_inc(S.s_own, 1)

    g.scalar.wait_ge(S.s_own, 1)
    g.scalar.dma_start(T.y[:, own], T.sum_own[:]).then_inc(S.st_own, 16)
    g.scalar.wait_ge(S.st_own, 16)
    g.sync.wait_ge(S.r_off, n_off)
    g.sync.dma_start(T.y[:, off], T.land_off[:]).then_inc(S.st_off, 16)
    g.sync.wait_ge(S.st_off, 16)
    g.wait_ge(S.sent, sent[0])
